import numpy as np
import ml_dtypes


def mxq(x, axis, fmt="e4m3"):
    dtype, down = {"e4m3": (ml_dtypes.float8_e4m3fn, 7), "e5m2": (ml_dtypes.float8_e5m2, 14)}[fmt]
    v = np.moveaxis(np.asarray(x, np.float32).astype(ml_dtypes.bfloat16).astype(np.float64), axis, -1)
    blocks = v.reshape(v.shape[:-1] + (-1, 32))
    amax = np.abs(blocks).max(-1, keepdims=True)
    byte = np.maximum(np.where(amax > 0, np.frexp(amax)[1] - 1 + 127, 0) - down, 1)
    scale = np.exp2(byte - 127.0)
    codes = (blocks / scale).astype(np.float32).astype(dtype).astype(np.float64)
    return np.moveaxis((codes * scale).reshape(v.shape), -1, axis)


WIDE = False


def mx_kscale(k):
    if not WIDE:
        return np.ones(k)
    levels = np.array([10, -10, 5, -5, 0])
    if k % 512:
        return np.exp2(np.random.permutation(np.resize(levels, k // 32))).repeat(32)
    a = np.empty((k // 512, 16))
    for p in range(k // 512):
        a[p, :8] = np.random.permutation(np.resize(levels, 8))
        for g in range(8):
            far = levels[np.abs(levels - a[p, g]) >= 10]
            a[p, g + 8] = far[np.random.randint(len(far))]
    return np.exp2(a.ravel()).repeat(32)


def f64(x):
    return np.asarray(x).astype(np.float64)


def striped(idx):
    return np.tile(idx.reshape(-1, 16).T, (8, 1)).astype(np.uint16)


def unstriped(offs):
    return offs[:16].T.reshape(-1).astype(np.int64)


def relu(v):
    return np.maximum(v, 0.0)


K, T, S, N = 512, 2048, 1024, 128


def setup_inputs():
    n = np.random.standard_normal
    s = mx_kscale(K)[:, None]
    return {
        "xT": (n((K, S)) * s).astype(np.float32),
        "w": (n((K, N)) / np.sqrt(K) / s).astype(np.float32),
        "b": (0.3 * n((N, 1))).astype(np.float32),
        "gate": np.tile(np.random.uniform(0.2, 1.0, S), (N, 1)).astype(np.float32),
        "offs": striped(np.random.permutation(T)[:S]),
    }


def reference(xT, w, b, gate, offs):
    idx = unstriped(offs)
    xq = mxq(f64(xT), 0, "e4m3")
    y = mxq(f64(w), 0, "e4m3").T @ xq
    y = relu(y + f64(b))
    out = np.zeros((N, T))
    out[:, idx] = f64(gate) * y
    return out

@@ -1,0 +1,140 @@
+from contextlib import ExitStack
+
+import concourse.mybir as mybir
+
+K, T, S, N = 512, 2048, 1024, 128
+FLOPS = 2 * K * S * N
+
+F32 = mybir.dt.float32
+BF16 = mybir.dt.bfloat16
+U32 = mybir.dt.uint32
+U16 = mybir.dt.uint16
+U8 = mybir.dt.uint8
+FP8X4 = mybir.dt.float8_e4m3fn_x4
+RELU = mybir.ActivationFunctionType.Relu
+MULT = mybir.AluOpType.mult
+
+P = 128
+PACK = 4
+CHUNK = 256
+CHUNKS = S // CHUNK
+VECTOR_COLUMNS = (160, 192, 112, 0)
+
+
+def interleave(copy, grouped, raw, first, last):
+    copy(
+        out=grouped[:, first:last, :].rearrange("p (c i) j -> p c j i", i=4),
+        in_=raw[:, :, first:last].rearrange("p j (c i) -> p c j i", i=4),
+    )
+
+
+def tile_picked_place_lin_relu_sub_l_kernel(tc, xT, w, b, gate, offs, out):
+    nc = tc.nc
+    with ExitStack() as ctx:
+        held = ctx.enter_context(tc.tile_pool(name="held", bufs=1))
+        psum = ctx.enter_context(tc.psum_pool(name="psum", bufs=1))
+
+        offsets = held.tile([P, S // 16], U16, name="offsets")
+        window = held.tile([P, T], F32, name="window", align_bytes=64)
+        bias = held.tile([P, 1], F32, name="bias")
+        warm = held.tile([P, 1], F32, name="warm")
+        gate_0 = held.tile([P, CHUNK], F32, name="gate_0", align_bytes=64)
+        gate_1 = held.tile([P, CHUNK], F32, name="gate_1", align_bytes=64)
+        gate_23 = held.tile([P, 2 * CHUNK], F32, name="gate_23", align_bytes=64)
+        gates = (gate_0[:], gate_1[:], gate_23[:, 0:CHUNK], gate_23[:, CHUNK : 2 * CHUNK])
+        w_raw = held.tile([P, PACK, N], F32, name="w_raw", align_bytes=64)
+        x_raw = [held.tile([P, PACK, CHUNK], F32, name=f"x_raw{c}", align_bytes=64) for c in range(CHUNKS)]
+
+        def load_x(c):
+            nc.sync.dma_start(
+                out=x_raw[c][:],
+                in_=xT[:, c * CHUNK : (c + 1) * CHUNK].rearrange("(p j) s -> p j s", j=PACK),
+            )
+
+        load_x(0)
+        nc.sync.dma_start(out=w_raw[:], in_=w.rearrange("(p j) m -> p j m", j=PACK))
+        nc.scalar.dma_start(out=bias[:], in_=b)
+        load_x(1)
+        nc.sync.dma_start(offsets[:], offs)
+        nc.sync.dma_start(out=gate_0[:], in_=gate[:, 0:CHUNK])
+        load_x(2)
+        load_x(3)
+        nc.sync.dma_start(out=gate_1[:], in_=gate[:, CHUNK : 2 * CHUNK])
+        nc.sync.dma_start(out=gate_23[:], in_=gate[:, 2 * CHUNK : S])
+
+        nc.vector.memset(warm[:], 0.0)
+        nc.scalar.activation(warm[:], warm[:], RELU)
+        nc.gpsimd.memset(window[:], 0.0)
+
+        w_grouped = held.tile([P, N, PACK], BF16, name="w_grouped", align_bytes=64)
+        w_codes = held.tile([P, N], U32, name="w_codes", align_bytes=64)
+        w_scales = held.tile([P, N], U8, name="w_scales", align_bytes=64)
+        interleave(nc.vector.tensor_copy, w_grouped, w_raw, 0, N)
+        nc.vector.quantize_mx(
+            out=w_codes[:].bitcast(FP8X4), scales=w_scales[:], in_=w_grouped[:].rearrange("p m j -> p (m j)")
+        )
+
+        x_grouped = [held.tile([P, CHUNK, PACK], BF16, name=f"x_grouped{c}", align_bytes=64) for c in range(CHUNKS)]
+        x_codes = [held.tile([P, CHUNK], U32, name=f"x_codes{c}", align_bytes=64) for c in range(CHUNKS)]
+        x_scales = [held.tile([P, CHUNK], U8, name=f"x_scales{c}", align_bytes=64) for c in range(CHUNKS)]
+        y = [held.tile([P, CHUNK], F32, name=f"y{c}", align_bytes=64) for c in range(CHUNKS)]
+        acc = [psum.tile([P, CHUNK], F32, name=f"acc{c}") for c in range(CHUNKS)]
+
+        def cast(c):
+            cut = VECTOR_COLUMNS[c]
+            if cut:
+                interleave(nc.vector.tensor_copy, x_grouped[c], x_raw[c], 0, cut)
+            if cut < CHUNK:
+                interleave(nc.scalar.copy, x_grouped[c], x_raw[c], cut, CHUNK)
+
+        def quantise(c):
+            nc.vector.quantize_mx(
+                out=x_codes[c][:].bitcast(FP8X4),
+                scales=x_scales[c][:],
+                in_=x_grouped[c][:].rearrange("p s j -> p (s j)"),
+            )
+
+        def multiply(c):
+            nc.tensor.matmul_mx(
+                out=acc[c][:],
+                lhsT=w_codes[:].bitcast(FP8X4),
+                lhsT_scale=w_scales[:],
+                rhs=x_codes[c][:].bitcast(FP8X4),
+                rhs_scale=x_scales[c][:],
+                start=True,
+                stop=True,
+            )
+
+        def rectify(c):
+            nc.scalar.activation(y[c][:], acc[c][:], RELU, bias=bias[:])
+
+        def scatter(c):
+            nc.vector.tensor_tensor(
+                window[:].indirect(offsets[:, c * CHUNK // 16 : (c + 1) * CHUNK // 16]),
+                y[c][:],
+                gates[c],
+                MULT,
+            )
+
+        cast(0)
+        quantise(0)
+        multiply(0)
+        cast(1)
+        quantise(1)
+        multiply(1)
+        rectify(0)
+        cast(2)
+        quantise(2)
+        multiply(2)
+        scatter(0)
+        rectify(1)
+        cast(3)
+        quantise(3)
+        multiply(3)
+        scatter(1)
+        rectify(2)
+        scatter(2)
+        rectify(3)
+        scatter(3)
+
+        nc.sync.dma_start(out=out, in_=window[:])

@@ -18,7 +18,7 @@ P = 128
 PACK = 4
 CHUNK = 256
 CHUNKS = S // CHUNK
-VECTOR_COLUMNS = (160, 192, 112, 0)
+VECTOR_COLUMNS = (136, 192, 0, 0)
 
 
 def interleave(copy, grouped, raw, first, last):
@@ -43,42 +43,51 @@ def tile_picked_place_lin_relu_sub_l_kernel(tc, xT, w, b, gate, offs, out):
         gate_23 = held.tile([P, 2 * CHUNK], F32, name="gate_23", align_bytes=64)
         gates = (gate_0[:], gate_1[:], gate_23[:, 0:CHUNK], gate_23[:, CHUNK : 2 * CHUNK])
         w_raw = held.tile([P, PACK, N], F32, name="w_raw", align_bytes=64)
-        x_raw = [held.tile([P, PACK, CHUNK], F32, name=f"x_raw{c}", align_bytes=64) for c in range(CHUNKS)]
+        x_flat = [held.tile([P, (PACK + 1) * CHUNK], F32, name=f"x_flat{c}", align_bytes=64) for c in range(CHUNKS)]
+        x_raw = [t[:, 0 : PACK * CHUNK].rearrange("p (j s) -> p j s", j=PACK) for t in x_flat]
 
         def load_x(c):
             nc.sync.dma_start(
-                out=x_raw[c][:],
+                out=x_raw[c],
                 in_=xT[:, c * CHUNK : (c + 1) * CHUNK].rearrange("(p j) s -> p j s", j=PACK),
             )
 
         load_x(0)
         nc.sync.dma_start(out=w_raw[:], in_=w.rearrange("(p j) m -> p j m", j=PACK))
-        nc.scalar.dma_start(out=bias[:], in_=b)
         load_x(1)
+        nc.sync.dma_start(out=bias[:], in_=b)
         nc.sync.dma_start(offsets[:], offs)
         nc.sync.dma_start(out=gate_0[:], in_=gate[:, 0:CHUNK])
         load_x(2)
-        load_x(3)
         nc.sync.dma_start(out=gate_1[:], in_=gate[:, CHUNK : 2 * CHUNK])
+        load_x(3)
         nc.sync.dma_start(out=gate_23[:], in_=gate[:, 2 * CHUNK : S])
 
         nc.vector.memset(warm[:], 0.0)
         nc.scalar.activation(warm[:], warm[:], RELU)
-        nc.gpsimd.memset(window[:], 0.0)
+        nc.vector.memset(window[:, 0 : T // 2], 0.0)
+        nc.gpsimd.memset(window[:, T // 2 : T], 0.0)
 
         w_grouped = held.tile([P, N, PACK], BF16, name="w_grouped", align_bytes=64)
         w_codes = held.tile([P, N], U32, name="w_codes", align_bytes=64)
         w_scales = held.tile([P, N], U8, name="w_scales", align_bytes=64)
-        interleave(nc.vector.tensor_copy, w_grouped, w_raw, 0, N)
-        nc.vector.quantize_mx(
-            out=w_codes[:].bitcast(FP8X4), scales=w_scales[:], in_=w_grouped[:].rearrange("p m j -> p (m j)")
-        )
 
         x_grouped = [held.tile([P, CHUNK, PACK], BF16, name=f"x_grouped{c}", align_bytes=64) for c in range(CHUNKS)]
         x_codes = [held.tile([P, CHUNK], U32, name=f"x_codes{c}", align_bytes=64) for c in range(CHUNKS)]
         x_scales = [held.tile([P, CHUNK], U8, name=f"x_scales{c}", align_bytes=64) for c in range(CHUNKS)]
-        y = [held.tile([P, CHUNK], F32, name=f"y{c}", align_bytes=64) for c in range(CHUNKS)]
+        y_last = held.tile([P, CHUNK], F32, name="y_last", align_bytes=64)
+        starts = [(PACK - 1) * CHUNK + cut for cut in VECTOR_COLUMNS]
+        y = [x_flat[c][:, starts[c] : starts[c] + CHUNK] for c in range(1, CHUNKS)] + [y_last[:]]
         acc = [psum.tile([P, CHUNK], F32, name=f"acc{c}") for c in range(CHUNKS)]
+
+        def cast_w():
+            interleave(nc.vector.tensor_copy, w_grouped, w_raw, 0, 80)
+            interleave(nc.scalar.copy, w_grouped, w_raw, 80, N)
+
+        def quantise_w():
+            nc.vector.quantize_mx(
+                out=w_codes[:].bitcast(FP8X4), scales=w_scales[:], in_=w_grouped[:].rearrange("p m j -> p (m j)")
+            )
 
         def cast(c):
             cut = VECTOR_COLUMNS[c]
@@ -106,32 +115,34 @@ def tile_picked_place_lin_relu_sub_l_kernel(tc, xT, w, b, gate, offs, out):
             )
 
         def rectify(c):
-            nc.scalar.activation(y[c][:], acc[c][:], RELU, bias=bias[:])
+            nc.scalar.activation(y[c], acc[c][:], RELU, bias=bias[:])
 
         def scatter(c):
             nc.vector.tensor_tensor(
                 window[:].indirect(offsets[:, c * CHUNK // 16 : (c + 1) * CHUNK // 16]),
-                y[c][:],
+                y[c],
                 gates[c],
                 MULT,
             )
 
         cast(0)
+        cast_w()
         quantise(0)
+        quantise_w()
         multiply(0)
         cast(1)
         quantise(1)
         multiply(1)
         rectify(0)
+        scatter(0)
         cast(2)
         quantise(2)
         multiply(2)
-        scatter(0)
         rectify(1)
+        scatter(1)
         cast(3)
         quantise(3)
         multiply(3)
-        scatter(1)
         rectify(2)
         scatter(2)
         rectify(3)

@@ -18,13 +18,13 @@ P = 128
 PACK = 4
 CHUNK = 256
 CHUNKS = S // CHUNK
-VECTOR_COLUMNS = (136, 192, 0, 0)
+PIECES = ((0, 256), (256, 256), (512, 128), (640, 128), (768, 128), (896, 128))
 
 
-def interleave(copy, grouped, raw, first, last):
+def interleave(copy, grouped, raw):
     copy(
-        out=grouped[:, first:last, :].rearrange("p (c i) j -> p c j i", i=4),
-        in_=raw[:, :, first:last].rearrange("p j (c i) -> p c j i", i=4),
+        out=grouped.rearrange("p (c i) j -> p c j i", i=4),
+        in_=raw.rearrange("p j (c i) -> p c j i", i=4),
     )
 
 
@@ -43,13 +43,19 @@ def tile_picked_place_lin_relu_sub_l_kernel(tc, xT, w, b, gate, offs, out):
         gate_23 = held.tile([P, 2 * CHUNK], F32, name="gate_23", align_bytes=64)
         gates = (gate_0[:], gate_1[:], gate_23[:, 0:CHUNK], gate_23[:, CHUNK : 2 * CHUNK])
         w_raw = held.tile([P, PACK, N], F32, name="w_raw", align_bytes=64)
-        x_flat = [held.tile([P, (PACK + 1) * CHUNK], F32, name=f"x_flat{c}", align_bytes=64) for c in range(CHUNKS)]
-        x_raw = [t[:, 0 : PACK * CHUNK].rearrange("p (j s) -> p j s", j=PACK) for t in x_flat]
+        x_flat = [
+            held.tile([P, PACK * width + CHUNK], F32, name=f"x_flat{n}", align_bytes=64)
+            for n, (first, width) in enumerate(PIECES)
+        ]
+        x_raw = [
+            x_flat[n][:, 0 : PACK * width].rearrange("p (j s) -> p j s", j=PACK)
+            for n, (first, width) in enumerate(PIECES)
+        ]
 
-        def load_x(c):
+        def load_x(n):
+            first, width = PIECES[n]
             nc.sync.dma_start(
-                out=x_raw[c],
-                in_=xT[:, c * CHUNK : (c + 1) * CHUNK].rearrange("(p j) s -> p j s", j=PACK),
+                out=x_raw[n], in_=xT[:, first : first + width].rearrange("(p j) s -> p j s", j=PACK)
             )
 
         load_x(0)
@@ -59,8 +65,10 @@ def tile_picked_place_lin_relu_sub_l_kernel(tc, xT, w, b, gate, offs, out):
         nc.sync.dma_start(offsets[:], offs)
         nc.sync.dma_start(out=gate_0[:], in_=gate[:, 0:CHUNK])
         load_x(2)
-        nc.sync.dma_start(out=gate_1[:], in_=gate[:, CHUNK : 2 * CHUNK])
         load_x(3)
+        nc.sync.dma_start(out=gate_1[:], in_=gate[:, CHUNK : 2 * CHUNK])
+        load_x(4)
+        load_x(5)
         nc.sync.dma_start(out=gate_23[:], in_=gate[:, 2 * CHUNK : S])
 
         nc.vector.memset(warm[:], 0.0)
@@ -76,46 +84,41 @@ def tile_picked_place_lin_relu_sub_l_kernel(tc, xT, w, b, gate, offs, out):
         x_codes = [held.tile([P, CHUNK], U32, name=f"x_codes{c}", align_bytes=64) for c in range(CHUNKS)]
         x_scales = [held.tile([P, CHUNK], U8, name=f"x_scales{c}", align_bytes=64) for c in range(CHUNKS)]
         y_last = held.tile([P, CHUNK], F32, name="y_last", align_bytes=64)
-        starts = [(PACK - 1) * CHUNK + cut for cut in VECTOR_COLUMNS]
-        y = [x_flat[c][:, starts[c] : starts[c] + CHUNK] for c in range(1, CHUNKS)] + [y_last[:]]
+        y = [x_flat[1][:, 960 : 960 + CHUNK], x_flat[3][:, 384 : 384 + CHUNK], x_flat[5][:, 384 : 384 + CHUNK], y_last[:]]
         acc = [psum.tile([P, CHUNK], F32, name=f"acc{c}") for c in range(CHUNKS)]
 
-        def cast_w():
-            interleave(nc.vector.tensor_copy, w_grouped, w_raw, 0, 80)
-            interleave(nc.scalar.copy, w_grouped, w_raw, 80, N)
+        def cast_w(copy, first, last):
+            interleave(copy, w_grouped[:, first:last, :], w_raw[:, :, first:last])
 
         def quantise_w():
             nc.vector.quantize_mx(
                 out=w_codes[:].bitcast(FP8X4), scales=w_scales[:], in_=w_grouped[:].rearrange("p m j -> p (m j)")
             )
 
-        def cast(c):
-            cut = VECTOR_COLUMNS[c]
-            if cut:
-                interleave(nc.vector.tensor_copy, x_grouped[c], x_raw[c], 0, cut)
-            if cut < CHUNK:
-                interleave(nc.scalar.copy, x_grouped[c], x_raw[c], cut, CHUNK)
+        def cast(copy, n, first, last):
+            c, start = divmod(PIECES[n][0], CHUNK)
+            interleave(copy, x_grouped[c][:, start + first : start + last, :], x_raw[n][:, :, first:last])
 
-        def quantise(c):
+        def quantise(c, first=0, last=CHUNK):
             nc.vector.quantize_mx(
-                out=x_codes[c][:].bitcast(FP8X4),
-                scales=x_scales[c][:],
-                in_=x_grouped[c][:].rearrange("p s j -> p (s j)"),
+                out=x_codes[c][:, first:last].bitcast(FP8X4),
+                scales=x_scales[c][:, first:last],
+                in_=x_grouped[c][:, first:last, :].rearrange("p s j -> p (s j)"),
             )
 
-        def multiply(c):
+        def multiply(c, first=0, last=CHUNK):
             nc.tensor.matmul_mx(
-                out=acc[c][:],
+                out=acc[c][:, first:last],
                 lhsT=w_codes[:].bitcast(FP8X4),
                 lhsT_scale=w_scales[:],
-                rhs=x_codes[c][:].bitcast(FP8X4),
-                rhs_scale=x_scales[c][:],
+                rhs=x_codes[c][:, first:last].bitcast(FP8X4),
+                rhs_scale=x_scales[c][:, first:last],
                 start=True,
                 stop=True,
             )
 
-        def rectify(c):
-            nc.scalar.activation(y[c], acc[c][:], RELU, bias=bias[:])
+        def rectify(c, first=0, last=CHUNK):
+            nc.scalar.activation(y[c][:, first:last], acc[c][:, first:last], RELU, bias=bias[:])
 
         def scatter(c):
             nc.vector.tensor_tensor(
@@ -125,22 +128,30 @@ def tile_picked_place_lin_relu_sub_l_kernel(tc, xT, w, b, gate, offs, out):
                 MULT,
             )
 
-        cast(0)
-        cast_w()
+        on_vector, on_scalar = nc.vector.tensor_copy, nc.scalar.copy
+        cast(on_vector, 0, 0, 136)
+        cast(on_scalar, 0, 136, 256)
+        cast_w(on_vector, 0, 80)
+        cast_w(on_scalar, 80, 128)
         quantise(0)
         quantise_w()
         multiply(0)
-        cast(1)
-        quantise(1)
+        cast(on_vector, 1, 0, 128)
+        cast(on_vector, 1, 128, 192)
+        cast(on_scalar, 1, 192, 256)
+        quantise(1, 0, 128)
+        quantise(1, 128, 256)
         multiply(1)
         rectify(0)
         scatter(0)
-        cast(2)
+        cast(on_scalar, 2, 0, 128)
+        cast(on_scalar, 3, 0, 128)
         quantise(2)
         multiply(2)
         rectify(1)
         scatter(1)
-        cast(3)
+        cast(on_scalar, 4, 0, 128)
+        cast(on_scalar, 5, 0, 128)
         quantise(3)
         multiply(3)
         rectify(2)

@@ -36,7 +36,9 @@ def tile_picked_place_lin_relu_sub_l_kernel(tc, xT, w, b, gate, offs, out):
 
         offsets = held.tile([P, S // 16], U16, name="offsets")
         window = held.tile([P, T], F32, name="window", align_bytes=64)
-        bias = held.tile([P, 1], F32, name="bias")
+        bias_rows = held.tile([P, 32], F32, name="bias_rows", align_bytes=64)
+        bias_turned = held.tile([P, 32], F32, name="bias_turned", align_bytes=64)
+        nc.vector.memset(bias_rows[:], 0.0)
         warm = held.tile([P, 1], F32, name="warm")
         gate_0 = held.tile([P, CHUNK], F32, name="gate_0", align_bytes=64)
         gate_1 = held.tile([P, CHUNK], F32, name="gate_1", align_bytes=64)
@@ -60,8 +62,8 @@ def tile_picked_place_lin_relu_sub_l_kernel(tc, xT, w, b, gate, offs, out):
 
         load_x(0)
         nc.sync.dma_start(out=w_raw[:], in_=w.rearrange("(p j) m -> p j m", j=PACK))
+        nc.sync.dma_start(out=bias_rows[0:P:32, :], in_=b.rearrange("(q r) one -> q (r one)", r=32))
         load_x(1)
-        nc.sync.dma_start(out=bias[:], in_=b)
         nc.sync.dma_start(offsets[:], offs)
         nc.sync.dma_start(out=gate_0[:], in_=gate[:, 0:CHUNK])
         load_x(2)
@@ -73,8 +75,7 @@ def tile_picked_place_lin_relu_sub_l_kernel(tc, xT, w, b, gate, offs, out):
 
         nc.vector.memset(warm[:], 0.0)
         nc.scalar.activation(warm[:], warm[:], RELU)
-        nc.vector.memset(window[:, 0 : T // 2], 0.0)
-        nc.gpsimd.memset(window[:, T // 2 : T], 0.0)
+        nc.vector.memset(window[:], 0.0)
 
         w_grouped = held.tile([P, N, PACK], BF16, name="w_grouped", align_bytes=64)
         w_codes = held.tile([P, N], U32, name="w_codes", align_bytes=64)
@@ -118,7 +119,7 @@ def tile_picked_place_lin_relu_sub_l_kernel(tc, xT, w, b, gate, offs, out):
             )
 
         def rectify(c, first=0, last=CHUNK):
-            nc.scalar.activation(y[c][:, first:last], acc[c][:, first:last], RELU, bias=bias[:])
+            nc.scalar.activation(y[c][:, first:last], acc[c][:, first:last], RELU, bias=bias_turned[:, 0:1])
 
         def scatter(c):
             nc.vector.tensor_tensor(
@@ -135,6 +136,7 @@ def tile_picked_place_lin_relu_sub_l_kernel(tc, xT, w, b, gate, offs, out):
         cast_w(on_scalar, 80, 128)
         quantise(0)
         quantise_w()
+        nc.vector.transpose(bias_turned[:], bias_rows[:])
         multiply(0)
         cast(on_vector, 1, 0, 128)
         cast(on_vector, 1, 128, 192)

@@ -54,16 +54,24 @@ def tile_picked_place_lin_relu_sub_l_kernel(tc, xT, w, b, gate, offs, out):
             for n, (first, width) in enumerate(PIECES)
         ]
 
+        def load_on_both(tile, rows):
+            nc.sync.dma_start(out=tile[:, 0:2, :], in_=rows[:, 0:2, :])
+            nc.scalar.dma_start(out=tile[:, 2:4, :], in_=rows[:, 2:4, :])
+
+        def load_x_on_both(n):
+            first, width = PIECES[n]
+            load_on_both(x_raw[n], xT[:, first : first + width].rearrange("(p j) s -> p j s", j=PACK))
+
         def load_x(n):
             first, width = PIECES[n]
             nc.sync.dma_start(
                 out=x_raw[n], in_=xT[:, first : first + width].rearrange("(p j) s -> p j s", j=PACK)
             )
 
-        load_x(0)
-        nc.sync.dma_start(out=w_raw[:], in_=w.rearrange("(p j) m -> p j m", j=PACK))
+        load_x_on_both(0)
+        load_on_both(w_raw[:], w.rearrange("(p j) m -> p j m", j=PACK))
         nc.sync.dma_start(out=bias_rows[0:P:32, :], in_=b.rearrange("(q r) one -> q (r one)", r=32))
-        load_x(1)
+        load_x_on_both(1)
         nc.sync.dma_start(offsets[:], offs)
         nc.sync.dma_start(out=gate_0[:], in_=gate[:, 0:CHUNK])
         load_x(2)

@@ -18,6 +18,8 @@ P = 128
 PACK = 4
 CHUNK = 256
 CHUNKS = S // CHUNK
+HELD = 32
+LEAD = CHUNK - HELD
 PIECES = ((0, 256), (256, 256), (512, 128), (640, 128), (768, 128), (896, 128))
 
 
@@ -46,11 +48,11 @@ def tile_picked_place_lin_relu_sub_l_kernel(tc, xT, w, b, gate, offs, out):
         gates = (gate_0[:], gate_1[:], gate_23[:, 0:CHUNK], gate_23[:, CHUNK : 2 * CHUNK])
         w_raw = held.tile([P, PACK, N], F32, name="w_raw", align_bytes=64)
         x_flat = [
-            held.tile([P, PACK * width + CHUNK], F32, name=f"x_flat{n}", align_bytes=64)
+            held.tile([P, LEAD + PACK * width], F32, name=f"x_flat{n}", align_bytes=64)
             for n, (first, width) in enumerate(PIECES)
         ]
         x_raw = [
-            x_flat[n][:, 0 : PACK * width].rearrange("p (j s) -> p j s", j=PACK)
+            x_flat[n][:, LEAD:].rearrange("p (j s) -> p j s", j=PACK)
             for n, (first, width) in enumerate(PIECES)
         ]
 
@@ -93,7 +95,7 @@ def tile_picked_place_lin_relu_sub_l_kernel(tc, xT, w, b, gate, offs, out):
         x_codes = [held.tile([P, CHUNK], U32, name=f"x_codes{c}", align_bytes=64) for c in range(CHUNKS)]
         x_scales = [held.tile([P, CHUNK], U8, name=f"x_scales{c}", align_bytes=64) for c in range(CHUNKS)]
         y_last = held.tile([P, CHUNK], F32, name="y_last", align_bytes=64)
-        y = [x_flat[1][:, 960 : 960 + CHUNK], x_flat[3][:, 384 : 384 + CHUNK], x_flat[5][:, 384 : 384 + CHUNK], y_last[:]]
+        y = [x_flat[1][:, 0:CHUNK], x_flat[3][:, 0:CHUNK], x_flat[5][:, 0:CHUNK], y_last[:]]
         acc = [psum.tile([P, CHUNK], F32, name=f"acc{c}") for c in range(CHUNKS)]
 
         def cast_w(copy, first, last):
@@ -146,23 +148,28 @@ def tile_picked_place_lin_relu_sub_l_kernel(tc, xT, w, b, gate, offs, out):
         quantise_w()
         nc.vector.transpose(bias_turned[:], bias_rows[:])
         multiply(0)
-        cast(on_vector, 1, 0, 128)
-        cast(on_vector, 1, 128, 192)
-        cast(on_scalar, 1, 192, 256)
-        quantise(1, 0, 128)
+        cast(on_vector, 1, 128, 256)
+        cast(on_vector, 1, 64, 128)
+        cast(on_scalar, 1, 0, 32)
+        cast(on_scalar, 1, 32, 64)
         quantise(1, 128, 256)
+        quantise(1, 0, 128)
         multiply(1)
         rectify(0)
         scatter(0)
         cast(on_scalar, 2, 0, 128)
-        cast(on_scalar, 3, 0, 128)
-        quantise(2)
+        cast(on_scalar, 3, 0, 64)
+        cast(on_scalar, 3, 64, 128)
+        quantise(2, 0, 128)
+        quantise(2, 128, 256)
         multiply(2)
         rectify(1)
         scatter(1)
         cast(on_scalar, 4, 0, 128)
-        cast(on_scalar, 5, 0, 128)
-        quantise(3)
+        cast(on_scalar, 5, 0, 64)
+        cast(on_scalar, 5, 64, 128)
+        quantise(3, 0, 128)
+        quantise(3, 128, 256)
         multiply(3)
         rectify(2)
         scatter(2)

@@ -74,8 +74,8 @@ def tile_picked_place_lin_relu_sub_l_kernel(tc, xT, w, b, gate, offs, out):
         load_on_both(w_raw[:], w.rearrange("(p j) m -> p j m", j=PACK))
         nc.sync.dma_start(out=bias_rows[0:P:32, :], in_=b.rearrange("(q r) one -> q (r one)", r=32))
         load_x_on_both(1)
-        nc.sync.dma_start(offsets[:], offs)
         nc.sync.dma_start(out=gate_0[:], in_=gate[:, 0:CHUNK])
+        nc.sync.dma_start(offsets[:], offs)
         load_x(2)
         load_x(3)
         nc.sync.dma_start(out=gate_1[:], in_=gate[:, CHUNK : 2 * CHUNK])

@@ -19,7 +19,7 @@ PACK = 4
 CHUNK = 256
 CHUNKS = S // CHUNK
 HELD = 32
-LEAD = CHUNK - HELD
+LEAD = CHUNK
 PIECES = ((0, 256), (256, 256), (512, 128), (640, 128), (768, 128), (896, 128))
 
 
@@ -36,19 +36,19 @@ def tile_picked_place_lin_relu_sub_l_kernel(tc, xT, w, b, gate, offs, out):
         held = ctx.enter_context(tc.tile_pool(name="held", bufs=1))
         psum = ctx.enter_context(tc.psum_pool(name="psum", bufs=1))
 
-        offsets = held.tile([P, S // 16], U16, name="offsets")
-        window = held.tile([P, T], F32, name="window", align_bytes=64)
+        offsets = held.tile([P, S // 16], U16, name="offsets", align_bytes=256)
+        window = held.tile([P, T], F32, name="window", align_bytes=256)
         bias_rows = held.tile([P, 32], F32, name="bias_rows", align_bytes=64)
         bias_turned = held.tile([P, 32], F32, name="bias_turned", align_bytes=64)
         nc.vector.memset(bias_rows[:], 0.0)
         warm = held.tile([P, 1], F32, name="warm")
-        gate_0 = held.tile([P, CHUNK], F32, name="gate_0", align_bytes=64)
-        gate_1 = held.tile([P, CHUNK], F32, name="gate_1", align_bytes=64)
-        gate_23 = held.tile([P, 2 * CHUNK], F32, name="gate_23", align_bytes=64)
+        gate_0 = held.tile([P, CHUNK], F32, name="gate_0", align_bytes=256)
+        gate_1 = held.tile([P, CHUNK], F32, name="gate_1", align_bytes=256)
+        gate_23 = held.tile([P, 2 * CHUNK], F32, name="gate_23", align_bytes=256)
         gates = (gate_0[:], gate_1[:], gate_23[:, 0:CHUNK], gate_23[:, CHUNK : 2 * CHUNK])
-        w_raw = held.tile([P, PACK, N], F32, name="w_raw", align_bytes=64)
+        w_raw = held.tile([P, PACK, N], F32, name="w_raw", align_bytes=256)
         x_flat = [
-            held.tile([P, LEAD + PACK * width], F32, name=f"x_flat{n}", align_bytes=64)
+            held.tile([P, LEAD + PACK * width], F32, name=f"x_flat{n}", align_bytes=256)
             for n, (first, width) in enumerate(PIECES)
         ]
         x_raw = [
@@ -95,7 +95,7 @@ def tile_picked_place_lin_relu_sub_l_kernel(tc, xT, w, b, gate, offs, out):
         x_codes = [held.tile([P, CHUNK], U32, name=f"x_codes{c}", align_bytes=64) for c in range(CHUNKS)]
         x_scales = [held.tile([P, CHUNK], U8, name=f"x_scales{c}", align_bytes=64) for c in range(CHUNKS)]
         y_last = held.tile([P, CHUNK], F32, name="y_last", align_bytes=64)
-        y = [x_flat[1][:, 0:CHUNK], x_flat[3][:, 0:CHUNK], x_flat[5][:, 0:CHUNK], y_last[:]]
+        y = [x_flat[n][:, HELD : HELD + CHUNK] for n in (1, 3, 5)] + [y_last[:]]
         acc = [psum.tile([P, CHUNK], F32, name=f"acc{c}") for c in range(CHUNKS)]
 
         def cast_w(copy, first, last):
@@ -160,16 +160,14 @@ def tile_picked_place_lin_relu_sub_l_kernel(tc, xT, w, b, gate, offs, out):
         cast(on_scalar, 2, 0, 128)
         cast(on_scalar, 3, 0, 64)
         cast(on_scalar, 3, 64, 128)
-        quantise(2, 0, 128)
-        quantise(2, 128, 256)
+        quantise(2)
         multiply(2)
         rectify(1)
         scatter(1)
         cast(on_scalar, 4, 0, 128)
         cast(on_scalar, 5, 0, 64)
         cast(on_scalar, 5, 64, 128)
-        quantise(3, 0, 128)
-        quantise(3, 128, 256)
+        quantise(3)
         multiply(3)
         rectify(2)
         scatter(2)

@@ -18,9 +18,9 @@ P = 128
 PACK = 4
 CHUNK = 256
 CHUNKS = S // CHUNK
-HELD = 32
-LEAD = CHUNK
-PIECES = ((0, 256), (256, 256), (512, 128), (640, 128), (768, 128), (896, 128))
+HALF = CHUNK // 2
+EDGE = 32
+PITCH = CHUNK + CHUNK - 2 * EDGE
 
 
 def interleave(copy, grouped, raw):
@@ -47,40 +47,49 @@ def tile_picked_place_lin_relu_sub_l_kernel(tc, xT, w, b, gate, offs, out):
         gate_23 = held.tile([P, 2 * CHUNK], F32, name="gate_23", align_bytes=256)
         gates = (gate_0[:], gate_1[:], gate_23[:, 0:CHUNK], gate_23[:, CHUNK : 2 * CHUNK])
         w_raw = held.tile([P, PACK, N], F32, name="w_raw", align_bytes=256)
-        x_flat = [
-            held.tile([P, LEAD + PACK * width], F32, name=f"x_flat{n}", align_bytes=256)
-            for n, (first, width) in enumerate(PIECES)
-        ]
-        x_raw = [
-            x_flat[n][:, LEAD:].rearrange("p (j s) -> p j s", j=PACK)
-            for n, (first, width) in enumerate(PIECES)
-        ]
+
+        def rows_of(columns):
+            return columns.rearrange("p (j s) -> p j s", j=PACK)
+
+        span = PACK * HALF
+        x_first = held.tile([P, PACK * CHUNK], F32, name="x_first", align_bytes=256)
+        x_second = held.tile([P, PACK * PITCH], F32, name="x_second", align_bytes=256)
+        x_front = [held.tile([P, span], F32, name=f"x_front{c}", align_bytes=256) for c in (2, 3)]
+        x_back = [held.tile([P, CHUNK + span], F32, name=f"x_back{c}", align_bytes=256) for c in (2, 3)]
+        y_last = held.tile([P, CHUNK], F32, name="y_last", align_bytes=64)
+        x_raw = {
+            (2, 0): rows_of(x_front[0][:]),
+            (2, 1): rows_of(x_back[0][:, CHUNK:]),
+            (3, 0): rows_of(x_front[1][:]),
+            (3, 1): rows_of(x_back[1][:, CHUNK:]),
+        }
+        x_first_rows = rows_of(x_first[:])
+        x_second_rows = rows_of(x_second[:])[:, :, 0:CHUNK]
+        y = [x_second[:, CHUNK - EDGE : 2 * CHUNK - EDGE]]
+        y.extend(tile[:, EDGE : EDGE + CHUNK] for tile in x_back)
+        y.append(y_last[:])
 
         def load_on_both(tile, rows):
             nc.sync.dma_start(out=tile[:, 0:2, :], in_=rows[:, 0:2, :])
             nc.scalar.dma_start(out=tile[:, 2:4, :], in_=rows[:, 2:4, :])
 
-        def load_x_on_both(n):
-            first, width = PIECES[n]
-            load_on_both(x_raw[n], xT[:, first : first + width].rearrange("(p j) s -> p j s", j=PACK))
+        x_rows = xT.rearrange("(p j) s -> p j s", j=PACK)
 
-        def load_x(n):
-            first, width = PIECES[n]
-            nc.sync.dma_start(
-                out=x_raw[n], in_=xT[:, first : first + width].rearrange("(p j) s -> p j s", j=PACK)
-            )
+        def load_half(c, h):
+            first = c * CHUNK + h * HALF
+            nc.sync.dma_start(out=x_raw[c, h], in_=x_rows[:, :, first : first + HALF])
 
-        load_x_on_both(0)
+        load_on_both(x_first_rows, x_rows[:, :, 0:CHUNK])
         load_on_both(w_raw[:], w.rearrange("(p j) m -> p j m", j=PACK))
         nc.sync.dma_start(out=bias_rows[0:P:32, :], in_=b.rearrange("(q r) one -> q (r one)", r=32))
-        load_x_on_both(1)
+        load_on_both(x_second_rows, x_rows[:, :, CHUNK : 2 * CHUNK])
         nc.sync.dma_start(out=gate_0[:], in_=gate[:, 0:CHUNK])
         nc.sync.dma_start(offsets[:], offs)
-        load_x(2)
-        load_x(3)
+        load_half(2, 0)
+        load_half(2, 1)
         nc.sync.dma_start(out=gate_1[:], in_=gate[:, CHUNK : 2 * CHUNK])
-        load_x(4)
-        load_x(5)
+        load_half(3, 0)
+        load_half(3, 1)
         nc.sync.dma_start(out=gate_23[:], in_=gate[:, 2 * CHUNK : S])
 
         nc.vector.memset(warm[:], 0.0)
@@ -94,8 +103,7 @@ def tile_picked_place_lin_relu_sub_l_kernel(tc, xT, w, b, gate, offs, out):
         x_grouped = [held.tile([P, CHUNK, PACK], BF16, name=f"x_grouped{c}", align_bytes=64) for c in range(CHUNKS)]
         x_codes = [held.tile([P, CHUNK], U32, name=f"x_codes{c}", align_bytes=64) for c in range(CHUNKS)]
         x_scales = [held.tile([P, CHUNK], U8, name=f"x_scales{c}", align_bytes=64) for c in range(CHUNKS)]
-        y_last = held.tile([P, CHUNK], F32, name="y_last", align_bytes=64)
-        y = [x_flat[n][:, HELD : HELD + CHUNK] for n in (1, 3, 5)] + [y_last[:]]
+        acc_low = psum.tile([P, HALF], F32, name="acc_low")
         acc = [psum.tile([P, CHUNK], F32, name=f"acc{c}") for c in range(CHUNKS)]
 
         def cast_w(copy, first, last):
@@ -106,9 +114,8 @@ def tile_picked_place_lin_relu_sub_l_kernel(tc, xT, w, b, gate, offs, out):
                 out=w_codes[:].bitcast(FP8X4), scales=w_scales[:], in_=w_grouped[:].rearrange("p m j -> p (m j)")
             )
 
-        def cast(copy, n, first, last):
-            c, start = divmod(PIECES[n][0], CHUNK)
-            interleave(copy, x_grouped[c][:, start + first : start + last, :], x_raw[n][:, :, first:last])
+        def cast(copy, c, rows, first, last, start=0):
+            interleave(copy, x_grouped[c][:, start + first : start + last, :], rows[:, :, first:last])
 
         def quantise(c, first=0, last=CHUNK):
             nc.vector.quantize_mx(
@@ -117,9 +124,9 @@ def tile_picked_place_lin_relu_sub_l_kernel(tc, xT, w, b, gate, offs, out):
                 in_=x_grouped[c][:, first:last, :].rearrange("p s j -> p (s j)"),
             )
 
-        def multiply(c, first=0, last=CHUNK):
+        def multiply(c, sums, first=0, last=CHUNK):
             nc.tensor.matmul_mx(
-                out=acc[c][:, first:last],
+                out=sums[:, first:last],
                 lhsT=w_codes[:].bitcast(FP8X4),
                 lhsT_scale=w_scales[:],
                 rhs=x_codes[c][:, first:last].bitcast(FP8X4),
@@ -128,8 +135,8 @@ def tile_picked_place_lin_relu_sub_l_kernel(tc, xT, w, b, gate, offs, out):
                 stop=True,
             )
 
-        def rectify(c, first=0, last=CHUNK):
-            nc.scalar.activation(y[c][:, first:last], acc[c][:, first:last], RELU, bias=bias_turned[:, 0:1])
+        def rectify(c, sums, first=0, last=CHUNK):
+            nc.scalar.activation(y[c][:, first:last], sums[:, first:last], RELU, bias=bias_turned[:, 0:1])
 
         def scatter(c):
             nc.vector.tensor_tensor(
@@ -140,38 +147,36 @@ def tile_picked_place_lin_relu_sub_l_kernel(tc, xT, w, b, gate, offs, out):
             )
 
         on_vector, on_scalar = nc.vector.tensor_copy, nc.scalar.copy
-        cast(on_vector, 0, 0, 136)
-        cast(on_scalar, 0, 136, 256)
+        cast(on_vector, 0, x_first_rows, 0, 136)
+        cast(on_scalar, 0, x_first_rows, 136, CHUNK)
         cast_w(on_vector, 0, 80)
-        cast_w(on_scalar, 80, 128)
+        cast_w(on_scalar, 80, N)
         quantise(0)
         quantise_w()
         nc.vector.transpose(bias_turned[:], bias_rows[:])
-        multiply(0)
-        cast(on_vector, 1, 128, 256)
-        cast(on_vector, 1, 64, 128)
-        cast(on_scalar, 1, 0, 32)
-        cast(on_scalar, 1, 32, 64)
-        quantise(1, 128, 256)
+        multiply(0, acc[0], HALF, CHUNK)
+        multiply(0, acc_low, 0, HALF)
+        cast(on_vector, 1, x_second_rows, EDGE, 128)
+        cast(on_vector, 1, x_second_rows, 128, 192)
+        cast(on_vector, 1, x_second_rows, 192, CHUNK - EDGE)
+        cast(on_scalar, 1, x_second_rows, 0, EDGE)
+        cast(on_scalar, 1, x_second_rows, CHUNK - EDGE, CHUNK)
         quantise(1, 0, 128)
-        multiply(1)
-        rectify(0)
+        quantise(1, 128, 192)
+        quantise(1, 192, CHUNK)
+        multiply(1, acc[1])
+        rectify(0, acc[0], HALF, CHUNK)
+        rectify(0, acc_low, 0, HALF)
         scatter(0)
-        cast(on_scalar, 2, 0, 128)
-        cast(on_scalar, 3, 0, 64)
-        cast(on_scalar, 3, 64, 128)
-        quantise(2)
-        multiply(2)
-        rectify(1)
-        scatter(1)
-        cast(on_scalar, 4, 0, 128)
-        cast(on_scalar, 5, 0, 64)
-        cast(on_scalar, 5, 64, 128)
-        quantise(3)
-        multiply(3)
-        rectify(2)
-        scatter(2)
-        rectify(3)
+        for c in (2, 3):
+            cast(on_scalar, c, x_raw[c, 0], 0, HALF)
+            cast(on_scalar, c, x_raw[c, 1], 0, HALF // 2, HALF)
+            cast(on_scalar, c, x_raw[c, 1], HALF // 2, HALF, HALF)
+            quantise(c)
+            multiply(c, acc[c])
+            rectify(c - 1, acc[c - 1])
+            scatter(c - 1)
+        rectify(3, acc[3])
         scatter(3)
 
         nc.sync.dma_start(out=out, in_=window[:])

@@ -20,7 +20,7 @@ CHUNK = 256
 CHUNKS = S // CHUNK
 HALF = CHUNK // 2
 EDGE = 32
-PITCH = CHUNK + CHUNK - 2 * EDGE
+TAIL = 16
 
 
 def interleave(copy, grouped, raw):
@@ -53,7 +53,7 @@ def tile_picked_place_lin_relu_sub_l_kernel(tc, xT, w, b, gate, offs, out):
 
         span = PACK * HALF
         x_first = held.tile([P, PACK * CHUNK], F32, name="x_first", align_bytes=256)
-        x_second = held.tile([P, PACK * PITCH], F32, name="x_second", align_bytes=256)
+        x_second = held.tile([P, PACK * CHUNK + CHUNK], F32, name="x_second", align_bytes=256)
         x_front = [held.tile([P, span], F32, name=f"x_front{c}", align_bytes=256) for c in (2, 3)]
         x_back = [held.tile([P, CHUNK + span], F32, name=f"x_back{c}", align_bytes=256) for c in (2, 3)]
         y_last = held.tile([P, CHUNK], F32, name="y_last", align_bytes=64)
@@ -64,8 +64,8 @@ def tile_picked_place_lin_relu_sub_l_kernel(tc, xT, w, b, gate, offs, out):
             (3, 1): rows_of(x_back[1][:, CHUNK:]),
         }
         x_first_rows = rows_of(x_first[:])
-        x_second_rows = rows_of(x_second[:])[:, :, 0:CHUNK]
-        y = [x_second[:, CHUNK - EDGE : 2 * CHUNK - EDGE]]
+        x_second_rows = rows_of(x_second[:, 0 : PACK * CHUNK])
+        y = [x_second[:, PACK * CHUNK - TAIL : PACK * CHUNK - TAIL + CHUNK]]
         y.extend(tile[:, EDGE : EDGE + CHUNK] for tile in x_back)
         y.append(y_last[:])
 
@@ -154,19 +154,17 @@ def tile_picked_place_lin_relu_sub_l_kernel(tc, xT, w, b, gate, offs, out):
         quantise(0)
         quantise_w()
         nc.vector.transpose(bias_turned[:], bias_rows[:])
-        multiply(0, acc[0], HALF, CHUNK)
         multiply(0, acc_low, 0, HALF)
-        cast(on_vector, 1, x_second_rows, EDGE, 128)
-        cast(on_vector, 1, x_second_rows, 128, 192)
-        cast(on_vector, 1, x_second_rows, 192, CHUNK - EDGE)
-        cast(on_scalar, 1, x_second_rows, 0, EDGE)
-        cast(on_scalar, 1, x_second_rows, CHUNK - EDGE, CHUNK)
-        quantise(1, 0, 128)
-        quantise(1, 128, 192)
-        quantise(1, 192, CHUNK)
+        multiply(0, acc[0], HALF, CHUNK)
+        for first in (0, 64, 128):
+            cast(on_vector, 1, x_second_rows, first, first + 64)
+        cast(on_scalar, 1, x_second_rows, CHUNK - TAIL, CHUNK)
+        cast(on_scalar, 1, x_second_rows, 192, CHUNK - TAIL)
+        for first in (0, 64, 192, 128):
+            quantise(1, first, first + 64)
         multiply(1, acc[1])
-        rectify(0, acc[0], HALF, CHUNK)
         rectify(0, acc_low, 0, HALF)
+        rectify(0, acc[0], HALF, CHUNK)
         scatter(0)
         for c in (2, 3):
             cast(on_scalar, c, x_raw[c, 0], 0, HALF)

@@ -12,15 +12,18 @@ U16 = mybir.dt.uint16
 U8 = mybir.dt.uint8
 FP8X4 = mybir.dt.float8_e4m3fn_x4
 RELU = mybir.ActivationFunctionType.Relu
+COPY = mybir.ActivationFunctionType.Copy
 MULT = mybir.AluOpType.mult
+ADD = mybir.AluOpType.add
+MAX = mybir.AluOpType.max
 
 P = 128
 PACK = 4
 CHUNK = 256
 CHUNKS = S // CHUNK
 HALF = CHUNK // 2
-EDGE = 32
 TAIL = 16
+EDGE = 32
 
 
 def interleave(copy, grouped, raw):
@@ -45,29 +48,28 @@ def tile_picked_place_lin_relu_sub_l_kernel(tc, xT, w, b, gate, offs, out):
         gate_0 = held.tile([P, CHUNK], F32, name="gate_0", align_bytes=256)
         gate_1 = held.tile([P, CHUNK], F32, name="gate_1", align_bytes=256)
         gate_23 = held.tile([P, 2 * CHUNK], F32, name="gate_23", align_bytes=256)
-        gates = (gate_0[:], gate_1[:], gate_23[:, 0:CHUNK], gate_23[:, CHUNK : 2 * CHUNK])
         w_raw = held.tile([P, PACK, N], F32, name="w_raw", align_bytes=256)
 
         def rows_of(columns):
             return columns.rearrange("p (j s) -> p j s", j=PACK)
 
-        span = PACK * HALF
         x_first = held.tile([P, PACK * CHUNK], F32, name="x_first", align_bytes=256)
         x_second = held.tile([P, PACK * CHUNK + CHUNK], F32, name="x_second", align_bytes=256)
-        x_front = [held.tile([P, span], F32, name=f"x_front{c}", align_bytes=256) for c in (2, 3)]
-        x_back = [held.tile([P, CHUNK + span], F32, name=f"x_back{c}", align_bytes=256) for c in (2, 3)]
-        y_last = held.tile([P, CHUNK], F32, name="y_last", align_bytes=64)
-        x_raw = {
-            (2, 0): rows_of(x_front[0][:]),
-            (2, 1): rows_of(x_back[0][:, CHUNK:]),
-            (3, 0): rows_of(x_front[1][:]),
-            (3, 1): rows_of(x_back[1][:, CHUNK:]),
-        }
+        span = PACK * HALF
+        x_front = [held.tile([P, span], F32, name=f"x_front{c}", tag=f"front{c}", align_bytes=256) for c in (2, 3)]
+        x_back_2 = held.tile([P, CHUNK + span], F32, name="x_back2", align_bytes=256)
+        x_back_3 = held.tile([P, span], F32, name="x_back3", align_bytes=256)
+        y_1 = x_back_2[:, EDGE : EDGE + CHUNK]
+        weighed_1 = held.tile([P, CHUNK], F32, name="weighed_1", align_bytes=64)
         x_first_rows = rows_of(x_first[:])
         x_second_rows = rows_of(x_second[:, 0 : PACK * CHUNK])
-        y = [x_second[:, PACK * CHUNK - TAIL : PACK * CHUNK - TAIL + CHUNK]]
-        y.extend(tile[:, EDGE : EDGE + CHUNK] for tile in x_back)
-        y.append(y_last[:])
+        x_raw = {
+            (2, 0): rows_of(x_front[0][:]),
+            (2, 1): rows_of(x_back_2[:, CHUNK:]),
+            (3, 0): rows_of(x_front[1][:]),
+            (3, 1): rows_of(x_back_3[:]),
+        }
+        y = [x_second[:, PACK * CHUNK - TAIL : PACK * CHUNK - TAIL + CHUNK], y_1]
 
         def load_on_both(tile, rows):
             nc.sync.dma_start(out=tile[:, 0:2, :], in_=rows[:, 0:2, :])
@@ -100,10 +102,12 @@ def tile_picked_place_lin_relu_sub_l_kernel(tc, xT, w, b, gate, offs, out):
         w_codes = held.tile([P, N], U32, name="w_codes", align_bytes=64)
         w_scales = held.tile([P, N], U8, name="w_scales", align_bytes=64)
 
-        x_grouped = [held.tile([P, CHUNK, PACK], BF16, name=f"x_grouped{c}", align_bytes=64) for c in range(CHUNKS)]
-        x_codes = [held.tile([P, CHUNK], U32, name=f"x_codes{c}", align_bytes=64) for c in range(CHUNKS)]
+        x_grouped = [held.tile([P, CHUNK, PACK], BF16, name=f"x_grouped{c}", align_bytes=64) for c in range(3)]
+        last_front = held.tile([P, HALF, PACK], BF16, name="last_front", tag="front_then_results", align_bytes=64)
+        x_codes = {c: held.tile([P, CHUNK], U32, name=f"x_codes{c}", align_bytes=64) for c in (0, 1, 3)}
         x_scales = [held.tile([P, CHUNK], U8, name=f"x_scales{c}", align_bytes=64) for c in range(CHUNKS)]
         acc_low = psum.tile([P, HALF], F32, name="acc_low")
+        acc_low_3 = psum.tile([P, HALF], F32, name="acc_low_3")
         acc = [psum.tile([P, CHUNK], F32, name=f"acc{c}") for c in range(CHUNKS)]
 
         def cast_w(copy, first, last):
@@ -118,10 +122,13 @@ def tile_picked_place_lin_relu_sub_l_kernel(tc, xT, w, b, gate, offs, out):
             interleave(copy, x_grouped[c][:, start + first : start + last, :], rows[:, :, first:last])
 
         def quantise(c, first=0, last=CHUNK):
+            quantise_from(x_grouped[c][:, first:last, :], c, first, last)
+
+        def quantise_from(grouped, c, first, last):
             nc.vector.quantize_mx(
                 out=x_codes[c][:, first:last].bitcast(FP8X4),
                 scales=x_scales[c][:, first:last],
-                in_=x_grouped[c][:, first:last, :].rearrange("p s j -> p (s j)"),
+                in_=grouped.rearrange("p s j -> p (s j)"),
             )
 
         def multiply(c, sums, first=0, last=CHUNK):
@@ -138,12 +145,13 @@ def tile_picked_place_lin_relu_sub_l_kernel(tc, xT, w, b, gate, offs, out):
         def rectify(c, sums, first=0, last=CHUNK):
             nc.scalar.activation(y[c][:, first:last], sums[:, first:last], RELU, bias=bias_turned[:, 0:1])
 
-        def scatter(c):
-            nc.vector.tensor_tensor(
-                window[:].indirect(offsets[:, c * CHUNK // 16 : (c + 1) * CHUNK // 16]),
-                y[c],
-                gates[c],
-                MULT,
+        def places(first, last):
+            return window[:].indirect(offsets[:, first // 16 : last // 16])
+
+        def rectify_on_vector(y_23, c, sums, first=0, last=CHUNK):
+            start = (c - 2) * CHUNK
+            nc.vector.tensor_scalar(
+                y_23[:, start + first : start + last], sums[:, first:last], bias_turned[:, 0:1], 0.0, ADD, MAX
             )
 
         on_vector, on_scalar = nc.vector.tensor_copy, nc.scalar.copy
@@ -165,16 +173,28 @@ def tile_picked_place_lin_relu_sub_l_kernel(tc, xT, w, b, gate, offs, out):
         multiply(1, acc[1])
         rectify(0, acc_low, 0, HALF)
         rectify(0, acc[0], HALF, CHUNK)
-        scatter(0)
-        for c in (2, 3):
-            cast(on_scalar, c, x_raw[c, 0], 0, HALF)
-            cast(on_scalar, c, x_raw[c, 1], 0, HALF // 2, HALF)
-            cast(on_scalar, c, x_raw[c, 1], HALF // 2, HALF, HALF)
-            quantise(c)
-            multiply(c, acc[c])
-            rectify(c - 1, acc[c - 1])
-            scatter(c - 1)
-        rectify(3, acc[3])
-        scatter(3)
+        nc.vector.tensor_tensor(places(0, CHUNK), y[0], gate_0[:], MULT)
+        cast(on_scalar, 2, x_raw[2, 0], 0, HALF)
+        cast(on_scalar, 2, x_raw[2, 1], 0, HALF // 2, HALF)
+        rectify(1, acc[1])
+        cast(on_scalar, 2, x_raw[2, 1], HALF // 2, HALF, HALF)
+        interleave(on_scalar, last_front[:], x_raw[3, 0])
+        nc.vector.tensor_tensor(weighed_1[:], y_1, gate_1[:], MULT)
+        nc.scalar.activation(places(CHUNK, 2 * CHUNK), weighed_1[:], COPY)
+        codes_2 = held.tile([P, CHUNK], U32, name="x_codes2", tag="front3", align_bytes=256)
+        x_codes.setdefault(2, codes_2)
+        quantise(2)
+        last_back = held.tile([P, HALF, PACK], BF16, name="last_back", align_bytes=64)
+        interleave(on_vector, last_back[:], x_raw[3, 1])
+        quantise_from(last_front[:], 3, 0, HALF)
+        quantise_from(last_back[:], 3, HALF, CHUNK)
+        multiply(2, acc[2])
+        multiply(3, acc_low_3, 0, HALF)
+        multiply(3, acc[3], HALF, CHUNK)
+        y_23 = held.tile([P, 2 * CHUNK], F32, name="y_23", tag="front_then_results", align_bytes=64)
+        rectify_on_vector(y_23, 2, acc[2])
+        rectify_on_vector(y_23, 3, acc_low_3, 0, HALF)
+        rectify_on_vector(y_23, 3, acc[3], HALF, CHUNK)
+        nc.vector.tensor_tensor(places(2 * CHUNK, S), y_23[:], gate_23[:], MULT)
 
         nc.sync.dma_start(out=out, in_=window[:])

@@ -56,17 +56,18 @@ def tile_picked_place_lin_relu_sub_l_kernel(tc, xT, w, b, gate, offs, out):
         x_first = held.tile([P, PACK * CHUNK], F32, name="x_first", align_bytes=256)
         x_second = held.tile([P, PACK * CHUNK + CHUNK], F32, name="x_second", align_bytes=256)
         span = PACK * HALF
-        x_front = [held.tile([P, span], F32, name=f"x_front{c}", tag=f"front{c}", align_bytes=256) for c in (2, 3)]
-        x_back_2 = held.tile([P, CHUNK + span], F32, name="x_back2", align_bytes=256)
+        x_front_2 = held.tile([P, CHUNK + span], F32, name="x_front2", align_bytes=256)
+        x_front_3 = held.tile([P, span], F32, name="x_front3", align_bytes=256)
+        x_back_2 = held.tile([P, span], F32, name="x_back2", align_bytes=256)
         x_back_3 = held.tile([P, span], F32, name="x_back3", align_bytes=256)
-        y_1 = x_back_2[:, EDGE : EDGE + CHUNK]
+        y_1 = x_front_2[:, EDGE : EDGE + CHUNK]
         weighed_1 = held.tile([P, CHUNK], F32, name="weighed_1", align_bytes=64)
         x_first_rows = rows_of(x_first[:])
         x_second_rows = rows_of(x_second[:, 0 : PACK * CHUNK])
         x_raw = {
-            (2, 0): rows_of(x_front[0][:]),
-            (2, 1): rows_of(x_back_2[:, CHUNK:]),
-            (3, 0): rows_of(x_front[1][:]),
+            (2, 0): rows_of(x_front_2[:, CHUNK:]),
+            (2, 1): rows_of(x_back_2[:]),
+            (3, 0): rows_of(x_front_3[:]),
             (3, 1): rows_of(x_back_3[:]),
         }
         y = [x_second[:, PACK * CHUNK - TAIL : PACK * CHUNK - TAIL + CHUNK], y_1]
@@ -104,7 +105,7 @@ def tile_picked_place_lin_relu_sub_l_kernel(tc, xT, w, b, gate, offs, out):
 
         x_grouped = [held.tile([P, CHUNK, PACK], BF16, name=f"x_grouped{c}", align_bytes=64) for c in range(3)]
         last_front = held.tile([P, HALF, PACK], BF16, name="last_front", tag="front_then_results", align_bytes=64)
-        x_codes = {c: held.tile([P, CHUNK], U32, name=f"x_codes{c}", align_bytes=64) for c in (0, 1, 3)}
+        x_codes = [held.tile([P, CHUNK], U32, name=f"x_codes{c}", align_bytes=64) for c in range(CHUNKS)]
         x_scales = [held.tile([P, CHUNK], U8, name=f"x_scales{c}", align_bytes=64) for c in range(CHUNKS)]
         acc_low = psum.tile([P, HALF], F32, name="acc_low")
         acc_low_3 = psum.tile([P, HALF], F32, name="acc_low_3")
@@ -181,8 +182,6 @@ def tile_picked_place_lin_relu_sub_l_kernel(tc, xT, w, b, gate, offs, out):
         interleave(on_scalar, last_front[:], x_raw[3, 0])
         nc.vector.tensor_tensor(weighed_1[:], y_1, gate_1[:], MULT)
         nc.scalar.activation(places(CHUNK, 2 * CHUNK), weighed_1[:], COPY)
-        codes_2 = held.tile([P, CHUNK], U32, name="x_codes2", tag="front3", align_bytes=256)
-        x_codes.setdefault(2, codes_2)
         quantise(2)
         last_back = held.tile([P, HALF, PACK], BF16, name="last_back", align_bytes=64)
         interleave(on_vector, last_back[:], x_raw[3, 1])

@@ -24,6 +24,7 @@ CHUNKS = S // CHUNK
 HALF = CHUNK // 2
 TAIL = 16
 EDGE = 32
+LAST = 64
 
 
 def interleave(copy, grouped, raw):
@@ -109,6 +110,7 @@ def tile_picked_place_lin_relu_sub_l_kernel(tc, xT, w, b, gate, offs, out):
         x_scales = [held.tile([P, CHUNK], U8, name=f"x_scales{c}", align_bytes=64) for c in range(CHUNKS)]
         acc_low = psum.tile([P, HALF], F32, name="acc_low")
         acc_low_3 = psum.tile([P, HALF], F32, name="acc_low_3")
+        acc_mid_3 = psum.tile([P, CHUNK], F32, name="acc_mid_3")
         acc = [psum.tile([P, CHUNK], F32, name=f"acc{c}") for c in range(CHUNKS)]
 
         def cast_w(copy, first, last):
@@ -186,14 +188,17 @@ def tile_picked_place_lin_relu_sub_l_kernel(tc, xT, w, b, gate, offs, out):
         last_back = held.tile([P, HALF, PACK], BF16, name="last_back", align_bytes=64)
         interleave(on_vector, last_back[:], x_raw[3, 1])
         quantise_from(last_front[:], 3, 0, HALF)
-        quantise_from(last_back[:], 3, HALF, CHUNK)
+        quantise_from(last_back[:, 0:LAST, :], 3, HALF, CHUNK - LAST)
+        quantise_from(last_back[:, LAST:HALF, :], 3, CHUNK - LAST, CHUNK)
         multiply(2, acc[2])
         multiply(3, acc_low_3, 0, HALF)
-        multiply(3, acc[3], HALF, CHUNK)
+        multiply(3, acc_mid_3, HALF, CHUNK - LAST)
+        multiply(3, acc[3], CHUNK - LAST, CHUNK)
         y_23 = held.tile([P, 2 * CHUNK], F32, name="y_23", tag="front_then_results", align_bytes=64)
         rectify_on_vector(y_23, 2, acc[2])
         rectify_on_vector(y_23, 3, acc_low_3, 0, HALF)
-        rectify_on_vector(y_23, 3, acc[3], HALF, CHUNK)
+        rectify_on_vector(y_23, 3, acc_mid_3, HALF, CHUNK - LAST)
+        rectify_on_vector(y_23, 3, acc[3], CHUNK - LAST, CHUNK)
         nc.vector.tensor_tensor(places(2 * CHUNK, S), y_23[:], gate_23[:], MULT)
 
         nc.sync.dma_start(out=out, in_=window[:])

@@ -25,6 +25,7 @@ HALF = CHUNK // 2
 TAIL = 16
 EDGE = 32
 LAST = 64
+PIECES = (256, 256, 256, 256, 512, 512)
 
 
 def interleave(copy, grouped, raw):
@@ -41,7 +42,9 @@ def tile_picked_place_lin_relu_sub_l_kernel(tc, xT, w, b, gate, offs, out):
         psum = ctx.enter_context(tc.psum_pool(name="psum", bufs=1))
 
         offsets = held.tile([P, S // 16], U16, name="offsets", align_bytes=256)
-        window = held.tile([P, T], F32, name="window", align_bytes=256)
+        windows = [held.tile([P, T], F32, name=f"window{v}", align_bytes=256) for v in range(2)]
+        merged = held.tile([P, T], F32, name="merged", align_bytes=256)
+        zero = held.tile([P, 1], F32, name="zero")
         bias_rows = held.tile([P, 32], F32, name="bias_rows", align_bytes=64)
         bias_turned = held.tile([P, 32], F32, name="bias_turned", align_bytes=64)
         nc.vector.memset(bias_rows[:], 0.0)
@@ -98,7 +101,9 @@ def tile_picked_place_lin_relu_sub_l_kernel(tc, xT, w, b, gate, offs, out):
 
         nc.vector.memset(warm[:], 0.0)
         nc.scalar.activation(warm[:], warm[:], RELU)
-        nc.vector.memset(window[:], 0.0)
+        nc.vector.memset(zero[:], 0.0)
+        for window in windows:
+            nc.vector.tensor_copy(window[:], zero[:].to_broadcast([P, T]))
 
         w_grouped = held.tile([P, N, PACK], BF16, name="w_grouped", align_bytes=64)
         w_codes = held.tile([P, N], U32, name="w_codes", align_bytes=64)
@@ -148,14 +153,11 @@ def tile_picked_place_lin_relu_sub_l_kernel(tc, xT, w, b, gate, offs, out):
         def rectify(c, sums, first=0, last=CHUNK):
             nc.scalar.activation(y[c][:, first:last], sums[:, first:last], RELU, bias=bias_turned[:, 0:1])
 
-        def places(first, last):
-            return window[:].indirect(offsets[:, first // 16 : last // 16])
+        def places(v, c):
+            return windows[v][:].indirect(offsets[:, c * CHUNK // 16 : (c + 1) * CHUNK // 16])
 
-        def rectify_on_vector(y_23, c, sums, first=0, last=CHUNK):
-            start = (c - 2) * CHUNK
-            nc.vector.tensor_scalar(
-                y_23[:, start + first : start + last], sums[:, first:last], bias_turned[:, 0:1], 0.0, ADD, MAX
-            )
+        def rectify_on_vector(results, sums, first=0, last=CHUNK):
+            nc.vector.tensor_scalar(results[:, first:last], sums[:, first:last], bias_turned[:, 0:1], 0.0, ADD, MAX)
 
         on_vector, on_scalar = nc.vector.tensor_copy, nc.scalar.copy
         cast(on_vector, 0, x_first_rows, 0, 136)
@@ -176,14 +178,14 @@ def tile_picked_place_lin_relu_sub_l_kernel(tc, xT, w, b, gate, offs, out):
         multiply(1, acc[1])
         rectify(0, acc_low, 0, HALF)
         rectify(0, acc[0], HALF, CHUNK)
-        nc.vector.tensor_tensor(places(0, CHUNK), y[0], gate_0[:], MULT)
+        nc.vector.tensor_tensor(places(0, 0), y[0], gate_0[:], MULT)
         cast(on_scalar, 2, x_raw[2, 0], 0, HALF)
         cast(on_scalar, 2, x_raw[2, 1], 0, HALF // 2, HALF)
         rectify(1, acc[1])
         cast(on_scalar, 2, x_raw[2, 1], HALF // 2, HALF, HALF)
         interleave(on_scalar, last_front[:], x_raw[3, 0])
         nc.vector.tensor_tensor(weighed_1[:], y_1, gate_1[:], MULT)
-        nc.scalar.activation(places(CHUNK, 2 * CHUNK), weighed_1[:], COPY)
+        nc.scalar.activation(places(1, 1), weighed_1[:], COPY)
         quantise(2)
         last_back = held.tile([P, HALF, PACK], BF16, name="last_back", align_bytes=64)
         interleave(on_vector, last_back[:], x_raw[3, 1])
@@ -194,11 +196,20 @@ def tile_picked_place_lin_relu_sub_l_kernel(tc, xT, w, b, gate, offs, out):
         multiply(3, acc_low_3, 0, HALF)
         multiply(3, acc_mid_3, HALF, CHUNK - LAST)
         multiply(3, acc[3], CHUNK - LAST, CHUNK)
-        y_23 = held.tile([P, 2 * CHUNK], F32, name="y_23", tag="front_then_results", align_bytes=64)
-        rectify_on_vector(y_23, 2, acc[2])
-        rectify_on_vector(y_23, 3, acc_low_3, 0, HALF)
-        rectify_on_vector(y_23, 3, acc_mid_3, HALF, CHUNK - LAST)
-        rectify_on_vector(y_23, 3, acc[3], CHUNK - LAST, CHUNK)
-        nc.vector.tensor_tensor(places(2 * CHUNK, S), y_23[:], gate_23[:], MULT)
+        y_2 = held.tile([P, CHUNK], F32, name="y_2", tag="front_then_results", align_bytes=64)
+        y_3 = held.tile([P, CHUNK], F32, name="y_3", align_bytes=64)
+        weighed_2 = held.tile([P, CHUNK], F32, name="weighed_2", align_bytes=64)
+        rectify_on_vector(y_2, acc[2])
+        nc.vector.tensor_tensor(weighed_2[:], y_2[:], gate_23[:, 0:CHUNK], MULT)
+        nc.scalar.activation(places(0, 2), weighed_2[:], COPY)
+        rectify_on_vector(y_3, acc_low_3, 0, HALF)
+        rectify_on_vector(y_3, acc_mid_3, HALF, CHUNK - LAST)
+        rectify_on_vector(y_3, acc[3], CHUNK - LAST, CHUNK)
+        nc.vector.tensor_tensor(places(1, 3), y_3[:], gate_23[:, CHUNK:], MULT)
 
-        nc.sync.dma_start(out=out, in_=window[:])
+        first = 0
+        for width in PIECES:
+            piece = slice(first, first + width)
+            nc.vector.tensor_tensor(merged[:, piece], windows[0][:, piece], windows[1][:, piece], ADD)
+            nc.sync.dma_start(out=out[:, piece], in_=merged[:, piece])
+            first = first + width

@@ -25,7 +25,7 @@ HALF = CHUNK // 2
 TAIL = 16
 EDGE = 32
 LAST = 64
-PIECES = (256, 256, 256, 256, 512, 512)
+PIECES = (256, 256, 512, 512, 256, 256)
 
 
 def interleave(copy, grouped, raw):
@@ -208,8 +208,9 @@ def tile_picked_place_lin_relu_sub_l_kernel(tc, xT, w, b, gate, offs, out):
         nc.vector.tensor_tensor(places(1, 3), y_3[:], gate_23[:, CHUNK:], MULT)
 
         first = 0
-        for width in PIECES:
+        for turn, width in enumerate(PIECES):
             piece = slice(first, first + width)
             nc.vector.tensor_tensor(merged[:, piece], windows[0][:, piece], windows[1][:, piece], ADD)
-            nc.sync.dma_start(out=out[:, piece], in_=merged[:, piece])
+            queue = nc.scalar if turn % 2 else nc.sync
+            queue.dma_start(out=out[:, piece], in_=merged[:, piece])
             first = first + width

@@ -208,9 +208,8 @@ def tile_picked_place_lin_relu_sub_l_kernel(tc, xT, w, b, gate, offs, out):
         nc.vector.tensor_tensor(places(1, 3), y_3[:], gate_23[:, CHUNK:], MULT)
 
         first = 0
-        for turn, width in enumerate(PIECES):
+        for width in PIECES:
             piece = slice(first, first + width)
             nc.vector.tensor_tensor(merged[:, piece], windows[0][:, piece], windows[1][:, piece], ADD)
-            queue = nc.scalar if turn % 2 else nc.sync
-            queue.dma_start(out=out[:, piece], in_=merged[:, piece])
+            nc.sync.dma_start(out=out[:, piece], in_=merged[:, piece])
             first = first + width

from contextlib import ExitStack

import concourse.mybir as mybir

K, T, S, N = 512, 2048, 1024, 128
FLOPS = 2 * K * S * N

F32 = mybir.dt.float32
BF16 = mybir.dt.bfloat16
U32 = mybir.dt.uint32
U16 = mybir.dt.uint16
U8 = mybir.dt.uint8
FP8X4 = mybir.dt.float8_e4m3fn_x4
RELU = mybir.ActivationFunctionType.Relu
COPY = mybir.ActivationFunctionType.Copy
MULT = mybir.AluOpType.mult
ADD = mybir.AluOpType.add
MAX = mybir.AluOpType.max

P = 128
PACK = 4
CHUNK = 256
CHUNKS = S // CHUNK
HALF = CHUNK // 2
TAIL = 16
EDGE = 32
LAST = 64
PIECES = (256, 256, 512, 512, 256, 256)


def interleave(copy, grouped, raw):
    copy(
        out=grouped.rearrange("p (c i) j -> p c j i", i=4),
        in_=raw.rearrange("p j (c i) -> p c j i", i=4),
    )


def tile_picked_place_lin_relu_sub_l_kernel(tc, xT, w, b, gate, offs, out):
    nc = tc.nc
    with ExitStack() as ctx:
        held = ctx.enter_context(tc.tile_pool(name="held", bufs=1))
        psum = ctx.enter_context(tc.psum_pool(name="psum", bufs=1))

        offsets = held.tile([P, S // 16], U16, name="offsets", align_bytes=256)
        windows = [held.tile([P, T], F32, name=f"window{v}", align_bytes=256) for v in range(2)]
        merged = held.tile([P, T], F32, name="merged", align_bytes=256)
        zero = held.tile([P, 1], F32, name="zero")
        bias_rows = held.tile([P, 32], F32, name="bias_rows", align_bytes=64)
        bias_turned = held.tile([P, 32], F32, name="bias_turned", align_bytes=64)
        nc.vector.memset(bias_rows[:], 0.0)
        warm = held.tile([P, 1], F32, name="warm")
        gate_0 = held.tile([P, CHUNK], F32, name="gate_0", align_bytes=256)
        gate_1 = held.tile([P, CHUNK], F32, name="gate_1", align_bytes=256)
        gate_23 = held.tile([P, 2 * CHUNK], F32, name="gate_23", align_bytes=256)
        w_raw = held.tile([P, PACK, N], F32, name="w_raw", align_bytes=256)

        def rows_of(columns):
            return columns.rearrange("p (j s) -> p j s", j=PACK)

        x_first = held.tile([P, PACK * CHUNK], F32, name="x_first", align_bytes=256)
        x_second = held.tile([P, PACK * CHUNK + CHUNK], F32, name="x_second", align_bytes=256)
        span = PACK * HALF
        x_front_2 = held.tile([P, CHUNK + span], F32, name="x_front2", align_bytes=256)
        x_front_3 = held.tile([P, span], F32, name="x_front3", align_bytes=256)
        x_back_2 = held.tile([P, span], F32, name="x_back2", align_bytes=256)
        x_back_3 = held.tile([P, span], F32, name="x_back3", align_bytes=256)
        y_1 = x_front_2[:, EDGE : EDGE + CHUNK]
        weighed_1 = held.tile([P, CHUNK], F32, name="weighed_1", align_bytes=64)
        x_first_rows = rows_of(x_first[:])
        x_second_rows = rows_of(x_second[:, 0 : PACK * CHUNK])
        x_raw = {
            (2, 0): rows_of(x_front_2[:, CHUNK:]),
            (2, 1): rows_of(x_back_2[:]),
            (3, 0): rows_of(x_front_3[:]),
            (3, 1): rows_of(x_back_3[:]),
        }
        y = [x_second[:, PACK * CHUNK - TAIL : PACK * CHUNK - TAIL + CHUNK], y_1]

        def load_on_both(tile, rows):
            nc.sync.dma_start(out=tile[:, 0:2, :], in_=rows[:, 0:2, :])
            nc.scalar.dma_start(out=tile[:, 2:4, :], in_=rows[:, 2:4, :])

        x_rows = xT.rearrange("(p j) s -> p j s", j=PACK)

        def load_half(c, h):
            first = c * CHUNK + h * HALF
            nc.sync.dma_start(out=x_raw[c, h], in_=x_rows[:, :, first : first + HALF])

        load_on_both(x_first_rows, x_rows[:, :, 0:CHUNK])
        load_on_both(w_raw[:], w.rearrange("(p j) m -> p j m", j=PACK))
        nc.sync.dma_start(out=bias_rows[0:P:32, :], in_=b.rearrange("(q r) one -> q (r one)", r=32))
        load_on_both(x_second_rows, x_rows[:, :, CHUNK : 2 * CHUNK])
        nc.sync.dma_start(out=gate_0[:], in_=gate[:, 0:CHUNK])
        nc.sync.dma_start(offsets[:], offs)
        load_half(2, 0)
        load_half(2, 1)
        nc.sync.dma_start(out=gate_1[:], in_=gate[:, CHUNK : 2 * CHUNK])
        load_half(3, 0)
        load_half(3, 1)
        nc.sync.dma_start(out=gate_23[:], in_=gate[:, 2 * CHUNK : S])

        nc.vector.memset(warm[:], 0.0)
        nc.scalar.activation(warm[:], warm[:], RELU)
        nc.vector.memset(zero[:], 0.0)
        for window in windows:
            nc.vector.tensor_copy(window[:], zero[:].to_broadcast([P, T]))

        w_grouped = held.tile([P, N, PACK], BF16, name="w_grouped", align_bytes=64)
        w_codes = held.tile([P, N], U32, name="w_codes", align_bytes=64)
        w_scales = held.tile([P, N], U8, name="w_scales", align_bytes=64)

        x_grouped = [held.tile([P, CHUNK, PACK], BF16, name=f"x_grouped{c}", align_bytes=64) for c in range(3)]
        last_front = held.tile([P, HALF, PACK], BF16, name="last_front", tag="front_then_results", align_bytes=64)
        x_codes = [held.tile([P, CHUNK], U32, name=f"x_codes{c}", align_bytes=64) for c in range(CHUNKS)]
        x_scales = [held.tile([P, CHUNK], U8, name=f"x_scales{c}", align_bytes=64) for c in range(CHUNKS)]
        acc_low = psum.tile([P, HALF], F32, name="acc_low")
        acc_low_3 = psum.tile([P, HALF], F32, name="acc_low_3")
        acc_mid_3 = psum.tile([P, CHUNK], F32, name="acc_mid_3")
        acc = [psum.tile([P, CHUNK], F32, name=f"acc{c}") for c in range(CHUNKS)]

        def cast_w(copy, first, last):
            interleave(copy, w_grouped[:, first:last, :], w_raw[:, :, first:last])

        def quantise_w():
            nc.vector.quantize_mx(
                out=w_codes[:].bitcast(FP8X4), scales=w_scales[:], in_=w_grouped[:].rearrange("p m j -> p (m j)")
            )

        def cast(copy, c, rows, first, last, start=0):
            interleave(copy, x_grouped[c][:, start + first : start + last, :], rows[:, :, first:last])

        def quantise(c, first=0, last=CHUNK):
            quantise_from(x_grouped[c][:, first:last, :], c, first, last)

        def quantise_from(grouped, c, first, last):
            nc.vector.quantize_mx(
                out=x_codes[c][:, first:last].bitcast(FP8X4),
                scales=x_scales[c][:, first:last],
                in_=grouped.rearrange("p s j -> p (s j)"),
            )

        def multiply(c, sums, first=0, last=CHUNK):
            nc.tensor.matmul_mx(
                out=sums[:, first:last],
                lhsT=w_codes[:].bitcast(FP8X4),
                lhsT_scale=w_scales[:],
                rhs=x_codes[c][:, first:last].bitcast(FP8X4),
                rhs_scale=x_scales[c][:, first:last],
                start=True,
                stop=True,
            )

        def rectify(c, sums, first=0, last=CHUNK):
            nc.scalar.activation(y[c][:, first:last], sums[:, first:last], RELU, bias=bias_turned[:, 0:1])

        def places(v, c):
            return windows[v][:].indirect(offsets[:, c * CHUNK // 16 : (c + 1) * CHUNK // 16])

        def rectify_on_vector(results, sums, first=0, last=CHUNK):
            nc.vector.tensor_scalar(results[:, first:last], sums[:, first:last], bias_turned[:, 0:1], 0.0, ADD, MAX)

        on_vector, on_scalar = nc.vector.tensor_copy, nc.scalar.copy
        cast(on_vector, 0, x_first_rows, 0, 136)
        cast(on_scalar, 0, x_first_rows, 136, CHUNK)
        cast_w(on_vector, 0, 80)
        cast_w(on_scalar, 80, N)
        quantise(0)
        quantise_w()
        nc.vector.transpose(bias_turned[:], bias_rows[:])
        multiply(0, acc_low, 0, HALF)
        multiply(0, acc[0], HALF, CHUNK)
        for first in (0, 64, 128):
            cast(on_vector, 1, x_second_rows, first, first + 64)
        cast(on_scalar, 1, x_second_rows, CHUNK - TAIL, CHUNK)
        cast(on_scalar, 1, x_second_rows, 192, CHUNK - TAIL)
        for first in (0, 64, 192, 128):
            quantise(1, first, first + 64)
        multiply(1, acc[1])
        rectify(0, acc_low, 0, HALF)
        rectify(0, acc[0], HALF, CHUNK)
        nc.vector.tensor_tensor(places(0, 0), y[0], gate_0[:], MULT)
        cast(on_scalar, 2, x_raw[2, 0], 0, HALF)
        cast(on_scalar, 2, x_raw[2, 1], 0, HALF // 2, HALF)
        rectify(1, acc[1])
        cast(on_scalar, 2, x_raw[2, 1], HALF // 2, HALF, HALF)
        interleave(on_scalar, last_front[:], x_raw[3, 0])
        nc.vector.tensor_tensor(weighed_1[:], y_1, gate_1[:], MULT)
        nc.scalar.activation(places(1, 1), weighed_1[:], COPY)
        quantise(2)
        last_back = held.tile([P, HALF, PACK], BF16, name="last_back", align_bytes=64)
        interleave(on_vector, last_back[:], x_raw[3, 1])
        quantise_from(last_front[:], 3, 0, HALF)
        quantise_from(last_back[:, 0:LAST, :], 3, HALF, CHUNK - LAST)
        quantise_from(last_back[:, LAST:HALF, :], 3, CHUNK - LAST, CHUNK)
        multiply(2, acc[2])
        multiply(3, acc_low_3, 0, HALF)
        multiply(3, acc_mid_3, HALF, CHUNK - LAST)
        multiply(3, acc[3], CHUNK - LAST, CHUNK)
        y_2 = held.tile([P, CHUNK], F32, name="y_2", tag="front_then_results", align_bytes=64)
        y_3 = held.tile([P, CHUNK], F32, name="y_3", align_bytes=64)
        weighed_2 = held.tile([P, CHUNK], F32, name="weighed_2", align_bytes=64)
        rectify_on_vector(y_2, acc[2])
        nc.vector.tensor_tensor(weighed_2[:], y_2[:], gate_23[:, 0:CHUNK], MULT)
        nc.scalar.activation(places(0, 2), weighed_2[:], COPY)
        rectify_on_vector(y_3, acc_low_3, 0, HALF)
        rectify_on_vector(y_3, acc_mid_3, HALF, CHUNK - LAST)
        rectify_on_vector(y_3, acc[3], CHUNK - LAST, CHUNK)
        nc.vector.tensor_tensor(places(1, 3), y_3[:], gate_23[:, CHUNK:], MULT)

        first = 0
        for width in PIECES:
            piece = slice(first, first + width)
            nc.vector.tensor_tensor(merged[:, piece], windows[0][:, piece], windows[1][:, piece], ADD)
            nc.sync.dma_start(out=out[:, piece], in_=merged[:, piece])
            first = first + width
